import numpy as np
import ml_dtypes


def mxq(x, axis, fmt="e4m3"):
    dtype, down = {"e4m3": (ml_dtypes.float8_e4m3fn, 7), "e5m2": (ml_dtypes.float8_e5m2, 14)}[fmt]
    v = np.moveaxis(np.asarray(x, np.float32).astype(ml_dtypes.bfloat16).astype(np.float64), axis, -1)
    blocks = v.reshape(v.shape[:-1] + (-1, 32))
    amax = np.abs(blocks).max(-1, keepdims=True)
    byte = np.maximum(np.where(amax > 0, np.frexp(amax)[1] - 1 + 127, 0) - down, 1)
    scale = np.exp2(byte - 127.0)
    codes = (blocks / scale).astype(np.float32).astype(dtype).astype(np.float64)
    return np.moveaxis((codes * scale).reshape(v.shape), -1, axis)


WIDE = False


def mx_kscale(k):
    if not WIDE:
        return np.ones(k)
    levels = np.array([10, -10, 5, -5, 0])
    if k % 512:
        return np.exp2(np.random.permutation(np.resize(levels, k // 32))).repeat(32)
    a = np.empty((k // 512, 16))
    for p in range(k // 512):
        a[p, :8] = np.random.permutation(np.resize(levels, 8))
        for g in range(8):
            far = levels[np.abs(levels - a[p, g]) >= 10]
            a[p, g + 8] = far[np.random.randint(len(far))]
    return np.exp2(a.ravel()).repeat(32)


def f64(x):
    return np.asarray(x).astype(np.float64)


def striped(idx):
    return np.tile(idx.reshape(-1, 16).T, (8, 1)).astype(np.uint16)


def unstriped(offs):
    return offs[:16].T.reshape(-1).astype(np.int64)


E2M1 = np.array([0.0, 0.5, 1.0, 1.5, 2.0, 3.0, 4.0, 6.0, -0.0, -0.5, -1.0, -1.5, -2.0, -3.0, -4.0, -6.0])


def pack_weight(w, fmt):
    k, n = w.shape
    w = f64(np.asarray(w, np.float32).astype(ml_dtypes.bfloat16)).reshape(k // 32, 32, n)
    amax = np.abs(w).max(1)
    if fmt == "e4m3":
        byte = np.frexp(amax)[1] - 1 + 127 - 7
    else:
        mant, ex = np.frexp(amax / 6.0)
        byte = np.where(mant > 0.5, ex, ex - 1) + 127
    byte = np.clip(np.where(amax > 0, byte, 1), 1, 254)
    scaled = (w * np.exp2(127.0 - byte)[:, None, :]).reshape(k, n).astype(np.float32)
    by_word = np.ascontiguousarray(scaled.reshape(k // 512, 128, 4, n).transpose(0, 1, 3, 2))
    if fmt == "e4m3":
        words = by_word.astype(ml_dtypes.float8_e4m3fn).view(np.uint8)
    else:
        c = by_word.astype(ml_dtypes.float4_e2m1fn).view(np.uint8) & 0xF
        words = (c[..., 0::2] | (c[..., 1::2] << 4)).reshape(k // 512, 128, 2 * n)
    return np.ascontiguousarray(words), np.ascontiguousarray(byte.astype(np.uint8).reshape(k // 512, 16, n))


def unpack_weight(words, scales, fmt):
    g, _, n = scales.shape
    words = np.ascontiguousarray(words).reshape(g, 128, n, -1)
    if fmt == "e4m3":
        vals = words.view(ml_dtypes.float8_e4m3fn).astype(np.float64)
    else:
        nib = np.empty((g, 128, n, 4), np.uint8)
        nib[..., 0::2] = words & 0xF
        nib[..., 1::2] = words >> 4
        vals = E2M1[nib]
    vals = vals * np.repeat(np.exp2(scales.astype(np.float64) - 127.0), 8, axis=1)[..., None]
    return vals.transpose(0, 1, 3, 2).reshape(g * 512, n)


def gelu(v):
    return 0.5 * v * (1.0 + np.tanh(np.sqrt(2.0 / np.pi) * (v + 0.044715 * v**3)))


K, M, H, T, S, T3, S2, P = 1024, 512, 512, 4096, 1024, 2048, 1024, 512

def setup_inputs():
    n = np.random.standard_normal
    s = mx_kscale(K)[:, None]
    um = mx_kscale(M)[:, None]
    u = mx_kscale(H)[:, None]
    d = {}
    d["tab_words"], d["tab_scales"] = pack_weight(n((K, T)) * s, "e4m3")
    d["offs"] = striped(np.random.permutation(T)[:S])
    d["tab2_words"], d["tab2_scales"] = pack_weight(n((H, T3)) / H ** 0.5 / u, "e4m3")
    d["offs2"] = striped(np.random.permutation(T3)[:S2])
    d["pos1"] = striped(np.random.permutation(S)[:P])
    d["pos2"] = striped(np.random.permutation(S)[:P])
    d["w1_words"], d["w1_scales"] = pack_weight(2.2 * n((K, M)) / K ** 0.5 / s, "e2m1")
    d["gain"] = (np.exp(0.3 * n(M)) * um[:, 0]).astype(np.float32)
    d["w2"] = (2.5 * n((M, H)) / M ** 0.5 / um * u.T).astype(np.float32)
    d["w3_words"], d["w3_scales"] = pack_weight(0.8 * n((K, H)) / K ** 0.5 / s * u.T, "e4m3")
    d["age"] = (1.5 * n((S2, P))).astype(np.float32)
    return d

def reference(tab_words, tab_scales, offs, tab2_words, tab2_scales, offs2, pos1, pos2,
              w1_words, w1_scales, gain, w2, w3_words, w3_scales, age):
    v = unpack_weight(tab_words, tab_scales, "e4m3")[:, unstriped(offs)]
    v2 = unpack_weight(tab2_words, tab2_scales, "e4m3")[:, unstriped(offs2)]
    w1 = unpack_weight(w1_words, w1_scales, "e2m1")
    w3 = unpack_weight(w3_words, w3_scales, "e4m3")
    resp = 1.0 / (1.0 + np.exp(-(w1.T @ v)))
    b = f64(gain)[:, None] * resp
    h = mxq(f64(w2), 0, "e4m3").T @ mxq(b, 0, "e4m3") + w3.T @ v
    e = v2.T @ mxq(h, 0, "e4m3")
    return np.abs(e[:, unstriped(pos1)] + e[:, unstriped(pos2)] - f64(age))

@@ -1,0 +1,259 @@
+from contextlib import ExitStack
+
+import concourse.mybir as mybir
+
+K, M, H, T, S, T3, S2, PAIRS = 1024, 512, 512, 4096, 1024, 2048, 1024, 512
+FLOPS = 2 * S * (K * M + M * H + K * H + H * S2)
+
+F32 = mybir.dt.float32
+BF16 = mybir.dt.bfloat16
+I32 = mybir.dt.int32
+U32 = mybir.dt.uint32
+U16 = mybir.dt.uint16
+U8 = mybir.dt.uint8
+FP8X4 = mybir.dt.float8_e4m3fn_x4
+FP4X4 = mybir.dt.float4_e2m1fn_x4
+ACT = mybir.ActivationFunctionType
+ALU = mybir.AluOpType
+
+P = 128
+PACK = 4
+PASSES = K // (P * PACK)
+CHUNK = 128
+CHUNKS = S // CHUNK
+GROUPS = ((0, 2), (2, 2), (4, 2), (6, 1), (7, 1))
+BANK = 512
+HALVES = S // BANK
+ROW_TILES = S2 // P
+LIST_ROWS = 16
+
+
+def tile_list_hemifield_defect_scores_kernel(
+    tc, tab_words, tab_scales, offs, tab2_words, tab2_scales, offs2, pos1, pos2,
+    w1_words, w1_scales, gain, w2, w3_words, w3_scales, age, out,
+):
+    nc = tc.nc
+    with ExitStack() as ctx:
+        keep = ctx.enter_context(tc.tile_pool(name="keep", bufs=1))
+        ring = ctx.enter_context(tc.tile_pool(name="ring", bufs=2))
+        psum = ctx.enter_context(tc.psum_pool(name="psum", bufs=1))
+
+        def held(name, shape, dtype, tag=None):
+            return keep.tile(shape, dtype, name=name, tag=tag or name, align_bytes=64)
+
+        def bank(b, shape):
+            return psum.tile(shape, F32, name="bank%d" % b)
+
+        offs_t = held("offs_t", [P, S // LIST_ROWS], U16)
+        offs2_t = held("offs2_t", [P, S2 // LIST_ROWS], U16)
+        pos1_t = held("pos1_t", [P, PAIRS // LIST_ROWS], U16)
+        pos2_t = held("pos2_t", [P, PAIRS // LIST_ROWS], U16)
+
+        tab_w = [held("tab_w%d" % a, [P, T], U32) for a in range(PASSES)]
+        tab_s = held("tab_s", [P, T], U8)
+        tab2_w = held("tab2_w", [P, T3], U32)
+        tab2_s = held("tab2_s", [P, T3], U8)
+        w1_raw = held("w1_raw", [P, PASSES, M], U16)
+        w3_raw = held("w3_raw", [P, PASSES, H], U32)
+        w1s_raw = held("w1s_raw", [P, PASSES * M], U8)
+        w3s_raw = held("w3s_raw", [P, H], U8)
+        w2_raw = held("w2_raw", [P, PACK, H], F32)
+        gain_t = held("gain_t", [P, PACK], F32)
+        age_t = held("age_t", [P, ROW_TILES, PAIRS], F32)
+        v_s1 = held("v_s1", [P, S], U8)
+
+        for plane in (w1s_raw, tab_s):
+            nc.vector.memset(plane[:].bitcast(I32), 0)
+        for plane in (tab2_s, w3s_raw, v_s1):
+            nc.gpsimd.memset(plane[:].bitcast(I32), 0)
+
+        def load_w1_scales(q):
+            nc.sync.dma_start(
+                w1s_raw[32 * q : 32 * q + 4, :].bitcast(I32).rearrange("p (a c) -> p a c", a=PASSES),
+                w1_scales[:, 4 * q : 4 * q + 4, :].bitcast(I32).rearrange("a r c -> r a c"))
+
+        def load_tab2_scales(q):
+            nc.sync.dma_start(tab2_s[32 * q : 32 * q + 4, :].bitcast(I32),
+                              tab2_scales[0, 4 * q : 4 * q + 4, :].bitcast(I32))
+
+        def load_words(tile, words):
+            nc.sync.dma_start(tile[:].bitcast(I32), words.rearrange("p t i -> p (t i)").bitcast(I32))
+
+        nc.sync.dma_start(offs2_t[:], offs2)
+        nc.sync.dma_start(offs_t[:], offs)
+        nc.sync.dma_start(w1_raw[:].bitcast(I32), w1_words.bitcast(I32).rearrange("a p c -> p a c"))
+        load_w1_scales(0)
+        load_w1_scales(1)
+        load_words(tab2_w, tab2_words[0])
+        tab_rows = tab_scales.bitcast(I32).rearrange("a (q r) c -> r q a c", r=4)
+        for r in range(4):
+            nc.sync.dma_start(tab_s[r:P:16, :].bitcast(I32), tab_rows[r])
+        load_tab2_scales(0)
+        load_tab2_scales(1)
+        nc.sync.dma_start(w2_raw[:], w2.rearrange("(p j) c -> p j c", j=PACK))
+        load_tab2_scales(2)
+        load_tab2_scales(3)
+        load_w1_scales(2)
+        load_w1_scales(3)
+        load_words(tab_w[0], tab_words[0])
+        load_words(tab_w[1], tab_words[1])
+        nc.sync.dma_start(gain_t[:], gain.rearrange("(p t) -> p t", t=PACK))
+        for q in range(4):
+            nc.sync.dma_start(w3s_raw[32 * q : 32 * q + 8, :].bitcast(I32),
+                              w3_scales[:, 4 * q : 4 * q + 4, :].bitcast(I32))
+        nc.sync.dma_start(w3_raw[:].bitcast(I32),
+                          w3_words.rearrange("a p c i -> a p (c i)").bitcast(I32).rearrange("a p c -> p a c"))
+        nc.sync.dma_start(pos1_t[:], pos1)
+        nc.sync.dma_start(pos2_t[:], pos2)
+        age_rows = age.rearrange("(i p) j -> p i j", p=P)
+        for u in range(2):
+            nc.sync.dma_start(age_t[:, 4 * u : 4 * u + 4, :], age_rows[:, 4 * u : 4 * u + 4, :])
+
+        warm = held("warm", [P, PACK], F32)
+        nc.vector.memset(warm[:], 0.0)
+        nc.scalar.activation(warm[:], warm[:], ACT.Sigmoid)
+
+        w1_c = held("w1_c", [P, PASSES * M], U16)
+        nc.vector.tensor_copy(w1_c[:].rearrange("p (a t m) -> p a m t", a=PASSES, t=PACK),
+                              w1_raw[:].rearrange("p a (m t) -> p a m t", t=PACK))
+        v2_w = held("v2_w", [P, S2], U32)
+        nc.vector.tensor_copy(v2_w[:], tab2_w[:].indirect(offs2_t[:]))
+        v_s = held("v_s", [P, S], U8)
+        nc.vector.tensor_copy(v_s[:], tab_s[:].indirect(offs_t[:]))
+        nc.scalar.dma_start(v_s1[0:112, :].bitcast(I32), v_s[16:P, :].bitcast(I32))
+        v2_s = held("v2_s", [P, S2], U8)
+        nc.vector.tensor_copy(v2_s[:], tab2_s[:].indirect(offs2_t[:]))
+        w1_s = held("w1_s", [P, PASSES * M], U8)
+        nc.vector.tensor_copy(w1_s[:].rearrange("p (a t m) -> p a m t", a=PASSES, t=PACK),
+                              w1s_raw[:].rearrange("p (a m t) -> p a m t", a=PASSES, t=PACK))
+        w2_b = held("w2_b", [P, H * PACK], BF16)
+        nc.scalar.copy(w2_b[:].rearrange("p (t m j) -> p m j t", t=PACK, j=PACK),
+                              w2_raw[:].rearrange("p j (m t) -> p m j t", t=PACK))
+        w2_c = held("w2_c", [P, H], U32)
+        w2_s = held("w2_s", [P, H], U8)
+        nc.vector.quantize_mx(w2_c[:].bitcast(FP8X4), w2_s[:], w2_b[:])
+
+        v_w0 = held("v_w0", [P, S], U32)
+        v_w1 = held("v_w1", [P, S], U32)
+        per_half = BANK // LIST_ROWS
+
+        def pick_sectors(picked, a):
+            for hf in range(HALVES):
+                nc.vector.tensor_copy(picked[:, BANK * hf : BANK * (hf + 1)],
+                                      tab_w[a][:].indirect(offs_t[:, per_half * hf : per_half * (hf + 1)]))
+
+        pick_sectors(v_w0, 0)
+        pick_sectors(v_w1, 1)
+        v_w = (v_w0, v_w1)
+        v_planes = (v_s, v_s1)
+
+        def cols(c, n=1):
+            return slice(CHUNK * c, CHUNK * (c + n))
+
+        def slot(a, t):
+            return slice(M * a + P * t, M * a + P * (t + 1))
+
+        first_banks = [bank(c, [P, PACK, CHUNK]) for c in range(CHUNKS)]
+
+        def first_product(c, a):
+            for t in range(PACK):
+                nc.tensor.matmul_mx(
+                    first_banks[c][:, t, :],
+                    lhsT=w1_c[:, slot(a, t)].bitcast(FP4X4), lhsT_scale=w1_s[:, slot(a, t)],
+                    rhs=v_w[a][:, cols(c)].bitcast(FP8X4), rhs_scale=v_planes[a][:, cols(c)],
+                    start=(a == 0 and t == 0), stop=(a == PASSES - 1 and t == PACK - 1))
+
+        for a in range(PASSES):
+            for c in range(CHUNKS):
+                first_product(c, a)
+
+        w3_c = held("w3_c", [P, PASSES * H], U32)
+        nc.vector.tensor_copy(w3_c[:].rearrange("p (a t m) -> p a m t", a=PASSES, t=PACK),
+                              w3_raw[:].rearrange("p a (m t) -> p a m t", t=PACK))
+        w3_s = held("w3_s", [P, H], U8)
+        nc.vector.tensor_copy(w3_s[:].rearrange("p (t m) -> p m t", t=PACK),
+                              w3s_raw[:].rearrange("p (m t) -> p m t", t=PACK))
+        b_c = held("b_c", [P, S], U32)
+        b_s = held("b_s", [P, S], U8)
+        h_c = held("h_c", [P, S], U32)
+        h_s = held("h_s", [P, S], U8)
+        for g, (first, count) in enumerate(GROUPS):
+            width = count * CHUNK
+            resp = held("resp%d" % g, [P, width, PACK], F32)
+            for u in range(count):
+                nc.scalar.activation(resp[:, cols(u), :],
+                                     first_banks[first + u][:].rearrange("p t n -> p n t"), ACT.Sigmoid)
+            b_b = held("b_b%d" % g, [P, width, PACK], BF16)
+            nc.vector.tensor_tensor(b_b[:], resp[:], gain_t[:].unsqueeze(1).to_broadcast([P, width, PACK]), ALU.mult)
+            nc.vector.quantize_mx(b_c[:, cols(first, count)].bitcast(FP8X4), b_s[:, cols(first, count)],
+                                  b_b[:].rearrange("p n t -> p (n t)"))
+
+        for g, (first, count) in enumerate(GROUPS):
+            h_b = held("h_b%d" % g, [P, count * CHUNK, PACK], BF16)
+            for u in range(count):
+                c = first + u
+                acc = bank(c % 4, [P, PACK, CHUNK])
+                for a in range(PASSES):
+                    for t in range(PACK):
+                        nc.tensor.matmul_mx(
+                            acc[:, t, :],
+                            lhsT=w3_c[:, slot(a, t)].bitcast(FP8X4), lhsT_scale=w3_s[4 * a : P, slot(0, t)],
+                            rhs=v_w[a][:, cols(c)].bitcast(FP8X4), rhs_scale=v_planes[a][:, cols(c)],
+                            start=(a == 0 and t == 0), stop=False)
+                for t in range(PACK):
+                    nc.tensor.matmul_mx(
+                        acc[:, t, :],
+                        lhsT=w2_c[:, slot(0, t)].bitcast(FP8X4), lhsT_scale=w2_s[:, slot(0, t)],
+                        rhs=b_c[:, cols(c)].bitcast(FP8X4), rhs_scale=b_s[:, cols(c)],
+                        start=False, stop=(t == PACK - 1))
+                nc.scalar.copy(h_b[:, cols(u), :], acc[:].rearrange("p t n -> p n t"))
+            nc.vector.quantize_mx(h_c[:, cols(first, count)].bitcast(FP8X4), h_s[:, cols(first, count)],
+                                  h_b[:].rearrange("p n t -> p (n t)"))
+
+        scores, upper = {}, {}
+
+        def score(i):
+            scores[i] = ring.tile([P, S], F32, name="scores", bufs=4)
+            if i == 0:
+                plan = ((4, ((0, 4),)), (5, ((4, 2), (6, 1))), (6, ((7, 1),)))
+            elif i == 1:
+                plan = ((7, ((0, 4),)), (3, ((4, 4),)))
+            else:
+                plan = ((7 if i % 2 else 4, ((4, 4),)), (3 if i % 2 else 6, ((0, 4),)))
+            for b, runs in plan:
+                acc = bank(b, [P, BANK])
+                start = runs[0][0]
+                for first, count in runs:
+                    nc.tensor.matmul_mx(
+                        acc[:, cols(first - start, count)],
+                        lhsT=v2_w[:, cols(i)].bitcast(FP8X4), lhsT_scale=v2_s[:, cols(i)],
+                        rhs=h_c[:, cols(first, count)].bitcast(FP8X4), rhs_scale=h_s[:, cols(first, count)],
+                        start=True, stop=True)
+                total = sum(count for first, count in runs)
+                nc.scalar.copy(scores[i][:, cols(start, total)], acc[:, cols(0, total)])
+
+        def pick_upper(i):
+            upper[i] = held("upper%d" % i, [P, PAIRS], F32)
+            nc.vector.tensor_tensor(upper[i][:], scores[i][:].indirect(pos1_t[:]), age_t[:, i, :], ALU.subtract)
+
+        def finish(i):
+            pieces = 2 if i == ROW_TILES - 1 else 1
+            width = PAIRS // pieces
+            for u in range(pieces):
+                span = slice(width * u, width * (u + 1))
+                entries = pos2_t[:, width // LIST_ROWS * u : width // LIST_ROWS * (u + 1)]
+                total = age_t[:, (i + 1) % ROW_TILES, span]
+                nc.vector.tensor_tensor(total, scores[i][:].indirect(entries), upper[i][:, span], ALU.add)
+                result = ring.tile([P, width], F32, name="result", bufs=3)
+                nc.scalar.activation(result[:], total, ACT.Abs)
+                nc.sync.dma_start(out[P * i : P * (i + 1), span], result[:])
+
+        score(0)
+        score(1)
+        pick_upper(0)
+        for i in range(ROW_TILES):
+            if i + 2 < ROW_TILES:
+                score(i + 2)
+            if i + 1 < ROW_TILES:
+                pick_upper(i + 1)
+            finish(i)

@@ -88,21 +88,19 @@ def tile_list_hemifield_defect_scores_kernel(
         tab_rows = tab_scales.bitcast(I32).rearrange("a (q r) c -> r q a c", r=4)
         for r in range(4):
             nc.sync.dma_start(tab_s[r:P:16, :].bitcast(I32), tab_rows[r])
-        load_tab2_scales(0)
-        load_tab2_scales(1)
-        nc.sync.dma_start(w2_raw[:], w2.rearrange("(p j) c -> p j c", j=PACK))
-        load_tab2_scales(2)
-        load_tab2_scales(3)
         load_w1_scales(2)
         load_w1_scales(3)
         load_words(tab_w[0], tab_words[0])
+        for q in range(4):
+            load_tab2_scales(q)
+        nc.sync.dma_start(w2_raw[:], w2.rearrange("(p j) c -> p j c", j=PACK))
         load_words(tab_w[1], tab_words[1])
-        nc.sync.dma_start(gain_t[:], gain.rearrange("(p t) -> p t", t=PACK))
         for q in range(4):
             nc.sync.dma_start(w3s_raw[32 * q : 32 * q + 8, :].bitcast(I32),
                               w3_scales[:, 4 * q : 4 * q + 4, :].bitcast(I32))
         nc.sync.dma_start(w3_raw[:].bitcast(I32),
                           w3_words.rearrange("a p c i -> a p (c i)").bitcast(I32).rearrange("a p c -> p a c"))
+        nc.sync.dma_start(gain_t[:], gain.rearrange("(p t) -> p t", t=PACK))
         nc.sync.dma_start(pos1_t[:], pos1)
         nc.sync.dma_start(pos2_t[:], pos2)
         age_rows = age.rearrange("(i p) j -> p i j", p=P)
@@ -121,11 +119,20 @@ def tile_list_hemifield_defect_scores_kernel(
         v_s = held("v_s", [P, S], U8)
         nc.vector.tensor_copy(v_s[:], tab_s[:].indirect(offs_t[:]))
         nc.scalar.dma_start(v_s1[0:112, :].bitcast(I32), v_s[16:P, :].bitcast(I32))
-        v2_s = held("v2_s", [P, S2], U8)
-        nc.vector.tensor_copy(v2_s[:], tab2_s[:].indirect(offs2_t[:]))
         w1_s = held("w1_s", [P, PASSES * M], U8)
         nc.vector.tensor_copy(w1_s[:].rearrange("p (a t m) -> p a m t", a=PASSES, t=PACK),
                               w1s_raw[:].rearrange("p (a m t) -> p a m t", a=PASSES, t=PACK))
+        per_half = BANK // LIST_ROWS
+        v_w = {}
+
+        def pick_sectors(a, hf, tag=None):
+            v_w[a, hf] = held("v_w%d%d" % (a, hf), [P, BANK], U32, tag=tag)
+            nc.vector.tensor_copy(v_w[a, hf][:], tab_w[a][:].indirect(offs_t[:, per_half * hf : per_half * (hf + 1)]))
+
+        pick_sectors(0, 0)
+        v2_s = held("v2_s", [P, S2], U8)
+        nc.vector.tensor_copy(v2_s[:], tab2_s[:].indirect(offs2_t[:]))
+        pick_sectors(0, 1, tag="tab2_s")
         w2_b = held("w2_b", [P, H * PACK], BF16)
         nc.scalar.copy(w2_b[:].rearrange("p (t m j) -> p m j t", t=PACK, j=PACK),
                               w2_raw[:].rearrange("p j (m t) -> p m j t", t=PACK))
@@ -133,18 +140,8 @@ def tile_list_hemifield_defect_scores_kernel(
         w2_s = held("w2_s", [P, H], U8)
         nc.vector.quantize_mx(w2_c[:].bitcast(FP8X4), w2_s[:], w2_b[:])
 
-        v_w0 = held("v_w0", [P, S], U32)
-        v_w1 = held("v_w1", [P, S], U32)
-        per_half = BANK // LIST_ROWS
-
-        def pick_sectors(picked, a):
-            for hf in range(HALVES):
-                nc.vector.tensor_copy(picked[:, BANK * hf : BANK * (hf + 1)],
-                                      tab_w[a][:].indirect(offs_t[:, per_half * hf : per_half * (hf + 1)]))
-
-        pick_sectors(v_w0, 0)
-        pick_sectors(v_w1, 1)
-        v_w = (v_w0, v_w1)
+        pick_sectors(1, 0)
+        pick_sectors(1, 1)
         v_planes = (v_s, v_s1)
 
         def cols(c, n=1):
@@ -160,7 +157,7 @@ def tile_list_hemifield_defect_scores_kernel(
                 nc.tensor.matmul_mx(
                     first_banks[c][:, t, :],
                     lhsT=w1_c[:, slot(a, t)].bitcast(FP4X4), lhsT_scale=w1_s[:, slot(a, t)],
-                    rhs=v_w[a][:, cols(c)].bitcast(FP8X4), rhs_scale=v_planes[a][:, cols(c)],
+                    rhs=v_w[a, c // 4][:, cols(c % 4)].bitcast(FP8X4), rhs_scale=v_planes[a][:, cols(c)],
                     start=(a == 0 and t == 0), stop=(a == PASSES - 1 and t == PACK - 1))
 
         for a in range(PASSES):
@@ -198,7 +195,7 @@ def tile_list_hemifield_defect_scores_kernel(
                         nc.tensor.matmul_mx(
                             acc[:, t, :],
                             lhsT=w3_c[:, slot(a, t)].bitcast(FP8X4), lhsT_scale=w3_s[4 * a : P, slot(0, t)],
-                            rhs=v_w[a][:, cols(c)].bitcast(FP8X4), rhs_scale=v_planes[a][:, cols(c)],
+                            rhs=v_w[a, c // 4][:, cols(c % 4)].bitcast(FP8X4), rhs_scale=v_planes[a][:, cols(c)],
                             start=(a == 0 and t == 0), stop=False)
                 for t in range(PACK):
                     nc.tensor.matmul_mx(

@@ -234,16 +234,15 @@ def tile_list_hemifield_defect_scores_kernel(
             nc.vector.tensor_tensor(upper[i][:], scores[i][:].indirect(pos1_t[:]), age_t[:, i, :], ALU.subtract)
 
         def finish(i):
-            pieces = 2 if i == ROW_TILES - 1 else 1
-            width = PAIRS // pieces
-            for u in range(pieces):
-                span = slice(width * u, width * (u + 1))
-                entries = pos2_t[:, width // LIST_ROWS * u : width // LIST_ROWS * (u + 1)]
-                total = age_t[:, (i + 1) % ROW_TILES, span]
-                nc.vector.tensor_tensor(total, scores[i][:].indirect(entries), upper[i][:, span], ALU.add)
-                result = ring.tile([P, width], F32, name="result", bufs=3)
-                nc.scalar.activation(result[:], total, ACT.Abs)
-                nc.sync.dma_start(out[P * i : P * (i + 1), span], result[:])
+            edges = (0, 384, PAIRS) if i == ROW_TILES - 1 else (0, PAIRS)
+            total = held("total_last" if i == ROW_TILES - 1 else "total", [P, PAIRS], F32)
+            for left, right in zip(edges, edges[1:]):
+                entries = pos2_t[:, left // LIST_ROWS : right // LIST_ROWS]
+                nc.vector.tensor_tensor(total[:, left:right], scores[i][:].indirect(entries),
+                                        upper[i][:, left:right], ALU.add)
+                result = ring.tile([P, right - left], F32, name="result", bufs=3)
+                nc.scalar.activation(result[:], total[:, left:right], ACT.Abs)
+                nc.sync.dma_start(out[P * i : P * (i + 1), left:right], result[:])
 
         score(0)
         score(1)

from contextlib import ExitStack

import concourse.mybir as mybir

K, M, H, T, S, T3, S2, PAIRS = 1024, 512, 512, 4096, 1024, 2048, 1024, 512
FLOPS = 2 * S * (K * M + M * H + K * H + H * S2)

F32 = mybir.dt.float32
BF16 = mybir.dt.bfloat16
I32 = mybir.dt.int32
U32 = mybir.dt.uint32
U16 = mybir.dt.uint16
U8 = mybir.dt.uint8
FP8X4 = mybir.dt.float8_e4m3fn_x4
FP4X4 = mybir.dt.float4_e2m1fn_x4
ACT = mybir.ActivationFunctionType
ALU = mybir.AluOpType

P = 128
PACK = 4
PASSES = K // (P * PACK)
CHUNK = 128
CHUNKS = S // CHUNK
GROUPS = ((0, 2), (2, 2), (4, 2), (6, 1), (7, 1))
BANK = 512
HALVES = S // BANK
ROW_TILES = S2 // P
LIST_ROWS = 16


def tile_list_hemifield_defect_scores_kernel(
    tc, tab_words, tab_scales, offs, tab2_words, tab2_scales, offs2, pos1, pos2,
    w1_words, w1_scales, gain, w2, w3_words, w3_scales, age, out,
):
    nc = tc.nc
    with ExitStack() as ctx:
        keep = ctx.enter_context(tc.tile_pool(name="keep", bufs=1))
        ring = ctx.enter_context(tc.tile_pool(name="ring", bufs=2))
        psum = ctx.enter_context(tc.psum_pool(name="psum", bufs=1))

        def held(name, shape, dtype, tag=None):
            return keep.tile(shape, dtype, name=name, tag=tag or name, align_bytes=64)

        def bank(b, shape):
            return psum.tile(shape, F32, name="bank%d" % b)

        offs_t = held("offs_t", [P, S // LIST_ROWS], U16)
        offs2_t = held("offs2_t", [P, S2 // LIST_ROWS], U16)
        pos1_t = held("pos1_t", [P, PAIRS // LIST_ROWS], U16)
        pos2_t = held("pos2_t", [P, PAIRS // LIST_ROWS], U16)

        tab_w = [held("tab_w%d" % a, [P, T], U32) for a in range(PASSES)]
        tab_s = held("tab_s", [P, T], U8)
        tab2_w = held("tab2_w", [P, T3], U32)
        tab2_s = held("tab2_s", [P, T3], U8)
        w1_raw = held("w1_raw", [P, PASSES, M], U16)
        w3_raw = held("w3_raw", [P, PASSES, H], U32)
        w1s_raw = held("w1s_raw", [P, PASSES * M], U8)
        w3s_raw = held("w3s_raw", [P, H], U8)
        w2_raw = held("w2_raw", [P, PACK, H], F32)
        gain_t = held("gain_t", [P, PACK], F32)
        age_t = held("age_t", [P, ROW_TILES, PAIRS], F32)
        v_s1 = held("v_s1", [P, S], U8)

        for plane in (w1s_raw, tab_s):
            nc.vector.memset(plane[:].bitcast(I32), 0)
        for plane in (tab2_s, w3s_raw, v_s1):
            nc.gpsimd.memset(plane[:].bitcast(I32), 0)

        def load_w1_scales(q):
            nc.sync.dma_start(
                w1s_raw[32 * q : 32 * q + 4, :].bitcast(I32).rearrange("p (a c) -> p a c", a=PASSES),
                w1_scales[:, 4 * q : 4 * q + 4, :].bitcast(I32).rearrange("a r c -> r a c"))

        def load_tab2_scales(q):
            nc.sync.dma_start(tab2_s[32 * q : 32 * q + 4, :].bitcast(I32),
                              tab2_scales[0, 4 * q : 4 * q + 4, :].bitcast(I32))

        def load_words(tile, words):
            nc.sync.dma_start(tile[:].bitcast(I32), words.rearrange("p t i -> p (t i)").bitcast(I32))

        nc.sync.dma_start(offs2_t[:], offs2)
        nc.sync.dma_start(offs_t[:], offs)
        nc.sync.dma_start(w1_raw[:].bitcast(I32), w1_words.bitcast(I32).rearrange("a p c -> p a c"))
        load_w1_scales(0)
        load_w1_scales(1)
        load_words(tab2_w, tab2_words[0])
        tab_rows = tab_scales.bitcast(I32).rearrange("a (q r) c -> r q a c", r=4)
        for r in range(4):
            nc.sync.dma_start(tab_s[r:P:16, :].bitcast(I32), tab_rows[r])
        load_w1_scales(2)
        load_w1_scales(3)
        load_words(tab_w[0], tab_words[0])
        for q in range(4):
            load_tab2_scales(q)
        nc.sync.dma_start(w2_raw[:], w2.rearrange("(p j) c -> p j c", j=PACK))
        load_words(tab_w[1], tab_words[1])
        for q in range(4):
            nc.sync.dma_start(w3s_raw[32 * q : 32 * q + 8, :].bitcast(I32),
                              w3_scales[:, 4 * q : 4 * q + 4, :].bitcast(I32))
        nc.sync.dma_start(w3_raw[:].bitcast(I32),
                          w3_words.rearrange("a p c i -> a p (c i)").bitcast(I32).rearrange("a p c -> p a c"))
        nc.sync.dma_start(gain_t[:], gain.rearrange("(p t) -> p t", t=PACK))
        nc.sync.dma_start(pos1_t[:], pos1)
        nc.sync.dma_start(pos2_t[:], pos2)
        age_rows = age.rearrange("(i p) j -> p i j", p=P)
        for u in range(2):
            nc.sync.dma_start(age_t[:, 4 * u : 4 * u + 4, :], age_rows[:, 4 * u : 4 * u + 4, :])

        warm = held("warm", [P, PACK], F32)
        nc.vector.memset(warm[:], 0.0)
        nc.scalar.activation(warm[:], warm[:], ACT.Sigmoid)

        w1_c = held("w1_c", [P, PASSES * M], U16)
        nc.vector.tensor_copy(w1_c[:].rearrange("p (a t m) -> p a m t", a=PASSES, t=PACK),
                              w1_raw[:].rearrange("p a (m t) -> p a m t", t=PACK))
        v2_w = held("v2_w", [P, S2], U32)
        nc.vector.tensor_copy(v2_w[:], tab2_w[:].indirect(offs2_t[:]))
        v_s = held("v_s", [P, S], U8)
        nc.vector.tensor_copy(v_s[:], tab_s[:].indirect(offs_t[:]))
        nc.scalar.dma_start(v_s1[0:112, :].bitcast(I32), v_s[16:P, :].bitcast(I32))
        w1_s = held("w1_s", [P, PASSES * M], U8)
        nc.vector.tensor_copy(w1_s[:].rearrange("p (a t m) -> p a m t", a=PASSES, t=PACK),
                              w1s_raw[:].rearrange("p (a m t) -> p a m t", a=PASSES, t=PACK))
        per_half = BANK // LIST_ROWS
        v_w = {}

        def pick_sectors(a, hf, tag=None):
            v_w[a, hf] = held("v_w%d%d" % (a, hf), [P, BANK], U32, tag=tag)
            nc.vector.tensor_copy(v_w[a, hf][:], tab_w[a][:].indirect(offs_t[:, per_half * hf : per_half * (hf + 1)]))

        pick_sectors(0, 0)
        v2_s = held("v2_s", [P, S2], U8)
        nc.vector.tensor_copy(v2_s[:], tab2_s[:].indirect(offs2_t[:]))
        pick_sectors(0, 1, tag="tab2_s")
        w2_b = held("w2_b", [P, H * PACK], BF16)
        nc.scalar.copy(w2_b[:].rearrange("p (t m j) -> p m j t", t=PACK, j=PACK),
                              w2_raw[:].rearrange("p j (m t) -> p m j t", t=PACK))
        w2_c = held("w2_c", [P, H], U32)
        w2_s = held("w2_s", [P, H], U8)
        nc.vector.quantize_mx(w2_c[:].bitcast(FP8X4), w2_s[:], w2_b[:])

        pick_sectors(1, 0)
        pick_sectors(1, 1)
        v_planes = (v_s, v_s1)

        def cols(c, n=1):
            return slice(CHUNK * c, CHUNK * (c + n))

        def slot(a, t):
            return slice(M * a + P * t, M * a + P * (t + 1))

        first_banks = [bank(c, [P, PACK, CHUNK]) for c in range(CHUNKS)]

        def first_product(c, a):
            for t in range(PACK):
                nc.tensor.matmul_mx(
                    first_banks[c][:, t, :],
                    lhsT=w1_c[:, slot(a, t)].bitcast(FP4X4), lhsT_scale=w1_s[:, slot(a, t)],
                    rhs=v_w[a, c // 4][:, cols(c % 4)].bitcast(FP8X4), rhs_scale=v_planes[a][:, cols(c)],
                    start=(a == 0 and t == 0), stop=(a == PASSES - 1 and t == PACK - 1))

        for a in range(PASSES):
            for c in range(CHUNKS):
                first_product(c, a)

        w3_c = held("w3_c", [P, PASSES * H], U32)
        nc.vector.tensor_copy(w3_c[:].rearrange("p (a t m) -> p a m t", a=PASSES, t=PACK),
                              w3_raw[:].rearrange("p a (m t) -> p a m t", t=PACK))
        w3_s = held("w3_s", [P, H], U8)
        nc.vector.tensor_copy(w3_s[:].rearrange("p (t m) -> p m t", t=PACK),
                              w3s_raw[:].rearrange("p (m t) -> p m t", t=PACK))
        b_c = held("b_c", [P, S], U32)
        b_s = held("b_s", [P, S], U8)
        h_c = held("h_c", [P, S], U32)
        h_s = held("h_s", [P, S], U8)
        for g, (first, count) in enumerate(GROUPS):
            width = count * CHUNK
            resp = held("resp%d" % g, [P, width, PACK], F32)
            for u in range(count):
                nc.scalar.activation(resp[:, cols(u), :],
                                     first_banks[first + u][:].rearrange("p t n -> p n t"), ACT.Sigmoid)
            b_b = held("b_b%d" % g, [P, width, PACK], BF16)
            nc.vector.tensor_tensor(b_b[:], resp[:], gain_t[:].unsqueeze(1).to_broadcast([P, width, PACK]), ALU.mult)
            nc.vector.quantize_mx(b_c[:, cols(first, count)].bitcast(FP8X4), b_s[:, cols(first, count)],
                                  b_b[:].rearrange("p n t -> p (n t)"))

        for g, (first, count) in enumerate(GROUPS):
            h_b = held("h_b%d" % g, [P, count * CHUNK, PACK], BF16)
            for u in range(count):
                c = first + u
                acc = bank(c % 4, [P, PACK, CHUNK])
                for a in range(PASSES):
                    for t in range(PACK):
                        nc.tensor.matmul_mx(
                            acc[:, t, :],
                            lhsT=w3_c[:, slot(a, t)].bitcast(FP8X4), lhsT_scale=w3_s[4 * a : P, slot(0, t)],
                            rhs=v_w[a, c // 4][:, cols(c % 4)].bitcast(FP8X4), rhs_scale=v_planes[a][:, cols(c)],
                            start=(a == 0 and t == 0), stop=False)
                for t in range(PACK):
                    nc.tensor.matmul_mx(
                        acc[:, t, :],
                        lhsT=w2_c[:, slot(0, t)].bitcast(FP8X4), lhsT_scale=w2_s[:, slot(0, t)],
                        rhs=b_c[:, cols(c)].bitcast(FP8X4), rhs_scale=b_s[:, cols(c)],
                        start=False, stop=(t == PACK - 1))
                nc.scalar.copy(h_b[:, cols(u), :], acc[:].rearrange("p t n -> p n t"))
            nc.vector.quantize_mx(h_c[:, cols(first, count)].bitcast(FP8X4), h_s[:, cols(first, count)],
                                  h_b[:].rearrange("p n t -> p (n t)"))

        scores, upper = {}, {}

        def score(i):
            scores[i] = ring.tile([P, S], F32, name="scores", bufs=4)
            if i == 0:
                plan = ((4, ((0, 4),)), (5, ((4, 2), (6, 1))), (6, ((7, 1),)))
            elif i == 1:
                plan = ((7, ((0, 4),)), (3, ((4, 4),)))
            else:
                plan = ((7 if i % 2 else 4, ((4, 4),)), (3 if i % 2 else 6, ((0, 4),)))
            for b, runs in plan:
                acc = bank(b, [P, BANK])
                start = runs[0][0]
                for first, count in runs:
                    nc.tensor.matmul_mx(
                        acc[:, cols(first - start, count)],
                        lhsT=v2_w[:, cols(i)].bitcast(FP8X4), lhsT_scale=v2_s[:, cols(i)],
                        rhs=h_c[:, cols(first, count)].bitcast(FP8X4), rhs_scale=h_s[:, cols(first, count)],
                        start=True, stop=True)
                total = sum(count for first, count in runs)
                nc.scalar.copy(scores[i][:, cols(start, total)], acc[:, cols(0, total)])

        def pick_upper(i):
            upper[i] = held("upper%d" % i, [P, PAIRS], F32)
            nc.vector.tensor_tensor(upper[i][:], scores[i][:].indirect(pos1_t[:]), age_t[:, i, :], ALU.subtract)

        def finish(i):
            edges = (0, 384, PAIRS) if i == ROW_TILES - 1 else (0, PAIRS)
            total = held("total_last" if i == ROW_TILES - 1 else "total", [P, PAIRS], F32)
            for left, right in zip(edges, edges[1:]):
                entries = pos2_t[:, left // LIST_ROWS : right // LIST_ROWS]
                nc.vector.tensor_tensor(total[:, left:right], scores[i][:].indirect(entries),
                                        upper[i][:, left:right], ALU.add)
                result = ring.tile([P, right - left], F32, name="result", bufs=3)
                nc.scalar.activation(result[:], total[:, left:right], ACT.Abs)
                nc.sync.dma_start(out[P * i : P * (i + 1), left:right], result[:])

        score(0)
        score(1)
        pick_upper(0)
        for i in range(ROW_TILES):
            if i + 2 < ROW_TILES:
                score(i + 2)
            if i + 1 < ROW_TILES:
                pick_upper(i + 1)
            finish(i)
